import numpy as np
import ml_dtypes


def mxq(x, axis, fmt="e4m3"):
    dtype, down = {"e4m3": (ml_dtypes.float8_e4m3fn, 7), "e5m2": (ml_dtypes.float8_e5m2, 14)}[fmt]
    v = np.moveaxis(np.asarray(x, np.float32).astype(ml_dtypes.bfloat16).astype(np.float64), axis, -1)
    blocks = v.reshape(v.shape[:-1] + (-1, 32))
    amax = np.abs(blocks).max(-1, keepdims=True)
    byte = np.maximum(np.where(amax > 0, np.frexp(amax)[1] - 1 + 127, 0) - down, 1)
    scale = np.exp2(byte - 127.0)
    codes = (blocks / scale).astype(np.float32).astype(dtype).astype(np.float64)
    return np.moveaxis((codes * scale).reshape(v.shape), -1, axis)


WIDE = False


def mx_kscale(k):
    if not WIDE:
        return np.ones(k)
    levels = np.array([10, -10, 5, -5, 0])
    if k % 512:
        return np.exp2(np.random.permutation(np.resize(levels, k // 32))).repeat(32)
    a = np.empty((k // 512, 16))
    for p in range(k // 512):
        a[p, :8] = np.random.permutation(np.resize(levels, 8))
        for g in range(8):
            far = levels[np.abs(levels - a[p, g]) >= 10]
            a[p, g + 8] = far[np.random.randint(len(far))]
    return np.exp2(a.ravel()).repeat(32)


def f64(x):
    return np.asarray(x).astype(np.float64)


def striped(idx):
    return np.tile(idx.reshape(-1, 16).T, (8, 1)).astype(np.uint16)


def unstriped(offs):
    return offs[:16].T.reshape(-1).astype(np.int64)


E2M1 = np.array([0.0, 0.5, 1.0, 1.5, 2.0, 3.0, 4.0, 6.0, -0.0, -0.5, -1.0, -1.5, -2.0, -3.0, -4.0, -6.0])


def pack_weight(w, fmt):
    k, n = w.shape
    w = f64(np.asarray(w, np.float32).astype(ml_dtypes.bfloat16)).reshape(k // 32, 32, n)
    amax = np.abs(w).max(1)
    if fmt == "e4m3":
        byte = np.frexp(amax)[1] - 1 + 127 - 7
    else:
        mant, ex = np.frexp(amax / 6.0)
        byte = np.where(mant > 0.5, ex, ex - 1) + 127
    byte = np.clip(np.where(amax > 0, byte, 1), 1, 254)
    scaled = (w * np.exp2(127.0 - byte)[:, None, :]).reshape(k, n).astype(np.float32)
    by_word = np.ascontiguousarray(scaled.reshape(k // 512, 128, 4, n).transpose(0, 1, 3, 2))
    if fmt == "e4m3":
        words = by_word.astype(ml_dtypes.float8_e4m3fn).view(np.uint8)
    else:
        c = by_word.astype(ml_dtypes.float4_e2m1fn).view(np.uint8) & 0xF
        words = (c[..., 0::2] | (c[..., 1::2] << 4)).reshape(k // 512, 128, 2 * n)
    return np.ascontiguousarray(words), np.ascontiguousarray(byte.astype(np.uint8).reshape(k // 512, 16, n))


def unpack_weight(words, scales, fmt):
    g, _, n = scales.shape
    words = np.ascontiguousarray(words).reshape(g, 128, n, -1)
    if fmt == "e4m3":
        vals = words.view(ml_dtypes.float8_e4m3fn).astype(np.float64)
    else:
        nib = np.empty((g, 128, n, 4), np.uint8)
        nib[..., 0::2] = words & 0xF
        nib[..., 1::2] = words >> 4
        vals = E2M1[nib]
    vals = vals * np.repeat(np.exp2(scales.astype(np.float64) - 127.0), 8, axis=1)[..., None]
    return vals.transpose(0, 1, 3, 2).reshape(g * 512, n)


def gelu(v):
    return 0.5 * v * (1.0 + np.tanh(np.sqrt(2.0 / np.pi) * (v + 0.044715 * v**3)))


K, T, S, H, N, T2 = 1024, 4096, 1024, 1024, 512, 2048

def setup_inputs():
    n = np.random.standard_normal
    s = mx_kscale(K)[:, None]
    u = mx_kscale(H)[:, None]
    tab_words, tab_scales = pack_weight(n((K, T)) * s, "e4m3")
    wb_words, wb_scales = pack_weight(0.8 * n((K, H)) / np.sqrt(K) / s, "e2m1")
    return {
        "tab_words": tab_words, "tab_scales": tab_scales,
        "wa": (0.8 * n((K, H)) / np.sqrt(K) / s).astype(np.float32),
        "wb_words": wb_words, "wb_scales": wb_scales,
        "load": (0.7 * n((H, S))).astype(np.float32),
        "gain": (np.exp(0.3 * n(H)) * u[:, 0]).astype(np.float32),
        "wc": (1.5 * n((H, N)) / np.sqrt(H) / u).astype(np.float32),
        "d": (0.7 * n(N)).astype(np.float32),
        "wgo": np.exp(0.3 * n((128, S))).astype(np.float32),
        "offs": striped(np.random.permutation(T)[:S]),
        "offs2": striped(np.random.permutation(T)[:S]),
        "offs3": striped(np.random.permutation(T2)[:S]),
    }

def reference(tab_words, tab_scales, wa, wb_words, wb_scales, load, gain, wc, d, wgo, offs, offs2, offs3):
    TW = unpack_weight(tab_words, tab_scales, "e4m3")
    v = TW[:, unstriped(offs)]
    v2 = TW[:, unstriped(offs2)]
    wb = unpack_weight(wb_words, wb_scales, "e2m1")
    b = mxq(f64(wa), 0, "e4m3").T @ v + wb.T @ v2
    h = np.tanh(b + f64(load)) * f64(gain)[:, None]
    y = mxq(f64(wc), 0, "e4m3").T @ mxq(h, 0, "e4m3")
    y = np.exp(-np.abs(y + f64(d)[:, None]))
    out = np.zeros((N, T2))
    out[:, unstriped(offs3)] = np.tile(f64(wgo), (N // 128, 1)) * y
    return out

@@ -1,0 +1,261 @@
+from contextlib import ExitStack
+
+import concourse.mybir as mybir
+
+K, T, S, H, N, T2 = 1024, 4096, 1024, 1024, 512, 2048
+FLOPS = 2 * S * H * (2 * K + N)
+
+F32 = mybir.dt.float32
+BF16 = mybir.dt.bfloat16
+I32 = mybir.dt.int32
+U32 = mybir.dt.uint32
+U16 = mybir.dt.uint16
+U8 = mybir.dt.uint8
+FP8X4 = mybir.dt.float8_e4m3fn_x4
+FP4X4 = mybir.dt.float4_e2m1fn_x4
+ACT = mybir.ActivationFunctionType
+ALU = mybir.AluOpType
+
+P = 128
+PACK = 4
+PASS = P * PACK
+BANK = 512
+LANES = 16
+CHUNKS = ((0, 256), (256, 256), (512, 512))
+HALF = N // 2
+
+
+def tile_list_handover_row_scores_kernel(
+    tc, tab_words, tab_scales, wa, wb_words, wb_scales, load, gain, wc, d, wgo, offs, offs2, offs3, out
+):
+    nc = tc.nc
+    KP, RP = K // PASS, H // PASS
+
+    with ExitStack() as ctx:
+        keep = ctx.enter_context(tc.tile_pool(name="keep", bufs=1))
+        raw = ctx.enter_context(tc.tile_pool(name="raw", bufs=4))
+        ring2 = ctx.enter_context(tc.tile_pool(name="ring2", bufs=2))
+        sums = ctx.enter_context(tc.tile_pool(name="sums", bufs=6))
+        scores = ctx.enter_context(tc.tile_pool(name="scores", bufs=4))
+        psum1 = ctx.enter_context(tc.psum_pool(name="psum1", bufs=6))
+        psum2 = ctx.enter_context(tc.psum_pool(name="psum2", bufs=2))
+
+        def held(name, shape, dtype):
+            return keep.tile(shape, dtype, name=name, align_bytes=64)
+
+        lists = []
+        for name, src in (("idx", offs), ("idx2", offs2), ("idx3", offs3)):
+            tile = held(name, [P, S // LANES], U16)
+            nc.sync.dma_start(tile[:], src)
+            lists.append(tile)
+        idx, idx2, idx3 = lists
+        gain_sb = held("gain_sb", [P, RP, PACK], F32)
+        nc.sync.dma_start(gain_sb[:], gain.rearrange("(g p t) -> p g t", g=RP, t=PACK))
+        d_sb = held("d_sb", [P, N // P], F32)
+        with nc.allow_non_contiguous_dma(reason="one bias value a partition"):
+            nc.sync.dma_start(d_sb[:], d.rearrange("(i p) -> p i", p=P))
+
+        tab_s = held("tab_s", [P, T], U8)
+        nc.vector.memset(tab_s[:].bitcast(I32), 0)
+        for q in range(4):
+            nc.scalar.dma_start(
+                tab_s[32 * q : 32 * q + 4 * KP, :].bitcast(I32), tab_scales[:, 4 * q : 4 * q + 4, :].bitcast(I32)
+            )
+        wb_s_raw = held("wb_s_raw", [P, KP, H], U8)
+        nc.gpsimd.memset(wb_s_raw[:].bitcast(I32), 0)
+        v2_s_last = held("v2_s_last", [P, S], U8)
+        nc.gpsimd.memset(v2_s_last[:].bitcast(I32), 0)
+        pages = []
+        for i in range(N // P):
+            page = held("page%d" % i, [P, T2], F32)
+            (nc.vector, nc.gpsimd)[i % 2].memset(page[:], 0.0)
+            pages.append(page)
+
+        tab_w = [held("tab_w%d" % a, [P, T], U32) for a in range(KP)]
+        v_w = [held("v_w%d" % a, [P, S], U32) for a in range(KP)]
+        v2_w = [held("v2_w%d" % a, [P, S], U32) for a in range(KP)]
+        v_s = held("v_s", [P, S], U8)
+        v2_s = held("v2_s", [P, S], U8)
+
+        def load_table(a):
+            nc.sync.dma_start(tab_w[a][:].bitcast(I32), tab_words[a].rearrange("p t i -> p (t i)").bitcast(I32))
+
+        def gather(dst, window, offsets, j0, width):
+            nc.vector.tensor_copy(
+                dst[:, j0 : j0 + width], window[:].indirect(offsets[:, j0 // LANES : (j0 + width) // LANES])
+            )
+
+        wa_w, wa_s = {}, {}
+
+        def prepare_wa(a, g):
+            rows = raw.tile([P, PACK, PASS], F32, name="rows")
+            nc.sync.dma_start(
+                rows[:], wa[a * PASS : (a + 1) * PASS, g * PASS : (g + 1) * PASS].rearrange("(p i) c -> p i c", i=PACK)
+            )
+            rounded = ring2.tile([P, PASS * PACK], BF16, name="wa_rounded", align_bytes=64)
+            nc.scalar.copy(
+                rounded[:].rearrange("p (t m i) -> p m i t", t=PACK, i=PACK),
+                rows[:].rearrange("p i (m t) -> p m i t", t=PACK),
+            )
+            wa_w[a, g] = held("wa_w%d%d" % (a, g), [P, PASS], U32)
+            wa_s[a, g] = held("wa_s%d%d" % (a, g), [P, PASS], U8)
+            nc.vector.quantize_mx(wa_w[a, g][:].bitcast(FP8X4), wa_s[a, g][:], rounded[:])
+
+        wb_raw = held("wb_raw", [P, KP, 2 * H], U8)
+        wb_w, wb_s = {}, {}
+
+        def deal_wb(g):
+            wb_w[g] = held("wb_w%d" % g, [P, KP, 2 * PASS], U8)
+            wb_s[g] = held("wb_s%d" % g, [P, KP, PASS], U8)
+            nc.vector.tensor_copy(
+                wb_w[g][:].bitcast(U16).rearrange("p a (t m) -> p a m t", t=PACK),
+                wb_raw[:].bitcast(U16)[:, :, g * PASS : (g + 1) * PASS].rearrange("p a (m t) -> p a m t", t=PACK),
+            )
+            nc.vector.tensor_copy(
+                wb_s[g][:].rearrange("p a (t m) -> p a m t", t=PACK),
+                wb_s_raw[:, :, g * PASS : (g + 1) * PASS].rearrange("p a (m t) -> p a m t", t=PACK),
+            )
+
+        load_sb = {}
+
+        def load_load(c, g):
+            j0, width = CHUNKS[c]
+            if width == BANK:
+                tile = raw.tile([P, PACK, width], F32, name="rows")
+            else:
+                tile = held("load%d%d" % (c, g), [P, PACK, width], F32)
+            nc.sync.dma_start(
+                tile[:], load[g * PASS : (g + 1) * PASS, j0 : j0 + width].rearrange("(p t) j -> p t j", t=PACK)
+            )
+            load_sb[c, g] = tile
+
+        wc_w, wc_s = {}, {}
+
+        def prepare_wc(g, half):
+            rows = ring2.tile([P, PACK, HALF], F32, name="wc_rows")
+            nc.sync.dma_start(
+                rows[:], wc[g * PASS : (g + 1) * PASS, half * HALF : (half + 1) * HALF].rearrange("(p t) n -> p t n", t=PACK)
+            )
+            rounded = ring2.tile([P, HALF * PACK], BF16, name="wc_rounded", align_bytes=64)
+            nc.scalar.copy(
+                rounded[:].rearrange("p (c e t) -> p c t e", e=PACK, t=PACK),
+                rows[:].rearrange("p t (c e) -> p c t e", e=PACK),
+            )
+            wc_w[g, half] = held("wc_w%d%d" % (g, half), [P, HALF], U32)
+            wc_s[g, half] = held("wc_s%d%d" % (g, half), [P, HALF], U8)
+            nc.vector.quantize_mx(wc_w[g, half][:].bitcast(FP8X4), wc_s[g, half][:], rounded[:])
+
+        h_w, h_s = {}, {}
+
+        def hidden(c, g):
+            j0, width = CHUNKS[c]
+            cols = slice(j0, j0 + width)
+            per_bank = BANK // width
+            h_rows = ring2.tile([P, PACK, width], BF16, name="h_rows", align_bytes=64)
+            for t0 in range(0, PACK, per_bank):
+                b = psum1.tile([P, per_bank, width], F32, name="b")
+                passes = []
+                for a in range(KP):
+                    for t in range(t0, t0 + per_bank):
+                        m = slice(t * P, (t + 1) * P)
+                        passes.append((
+                            t, wb_w[g][:, a, 2 * t * P : 2 * (t + 1) * P].bitcast(FP4X4), wb_s[g][:, a, m],
+                            v2_w[a][:, cols], (v2_s, v2_s_last)[a][:, cols],
+                        ))
+                    for t in range(t0, t0 + per_bank):
+                        m = slice(t * P, (t + 1) * P)
+                        passes.append((
+                            t, wa_w[a, g][:, m].bitcast(FP8X4), wa_s[a, g][:, m], v_w[a][:, cols], v_s[4 * a :, cols],
+                        ))
+                for n, (t, w, w_scale, v, v_scale) in enumerate(passes):
+                    nc.tensor.matmul_mx(
+                        b[:, t - t0, :], lhsT=w, lhsT_scale=w_scale, rhs=v.bitcast(FP8X4), rhs_scale=v_scale,
+                        start=(n == 0), stop=(n == len(passes) - 1),
+                    )
+                x = sums.tile([P, per_bank, width], F32, name="x")
+                nc.vector.tensor_tensor(x[:], b[:], load_sb[c, g][:, t0 : t0 + per_bank, :], ALU.add)
+                nc.scalar.activation(x[:], x[:], ACT.Tanh)
+                for t in range(t0, t0 + per_bank):
+                    nc.scalar.activation(h_rows[:, t, :], x[:, t - t0, :], ACT.Copy, scale=gain_sb[:, g, t : t + 1])
+            h_woven = ring2.tile([P, width * PACK], BF16, name="h_woven", align_bytes=64)
+            nc.scalar.copy(
+                h_woven[:].rearrange("p (c e t) -> p c t e", e=PACK, t=PACK),
+                h_rows[:].rearrange("p t (c e) -> p c t e", e=PACK),
+            )
+            h_w[c, g] = held("h_w%d%d" % (c, g), [P, width], U32)
+            h_s[c, g] = held("h_s%d%d" % (c, g), [P, width], U8)
+            nc.vector.quantize_mx(h_w[c, g][:].bitcast(FP8X4), h_s[c, g][:], h_woven[:])
+
+        wgo_sb = held("wgo_sb", [P, S], F32)
+
+        def score(c, half):
+            j0, width = CHUNKS[c]
+            per_bank = BANK // width
+            for i0 in range(2 * half, 2 * half + 2, per_bank):
+                z = psum2.tile([P, per_bank, width], F32, name="z")
+                y = scores.tile([P, per_bank, width], F32, name="y")
+                for i in range(i0, i0 + per_bank):
+                    m = slice((i % 2) * P, (i % 2 + 1) * P)
+                    for g in range(RP):
+                        nc.tensor.matmul_mx(
+                            z[:, i - i0, :], lhsT=wc_w[g, half][:, m].bitcast(FP8X4), lhsT_scale=wc_s[g, half][:, m],
+                            rhs=h_w[c, g][:].bitcast(FP8X4), rhs_scale=h_s[c, g][:],
+                            start=(g == 0), stop=(g == RP - 1),
+                        )
+                for i in range(i0, i0 + per_bank):
+                    nc.scalar.activation(y[:, i - i0, :], z[:, i - i0, :], ACT.Abs, bias=d_sb[:, i : i + 1])
+                nc.scalar.activation(y[:], y[:], ACT.Exp, scale=-1.0)
+                for i in range(i0, i0 + per_bank):
+                    nc.vector.tensor_tensor(
+                        pages[i][:].indirect(idx3[:, j0 // LANES : (j0 + width) // LANES]),
+                        y[:, i - i0, :], wgo_sb[:, j0 : j0 + width], ALU.mult,
+                    )
+                    if c == len(CHUNKS) - 1:
+                        nc.sync.dma_start(out[i * P : (i + 1) * P, :], pages[i][:])
+
+        load_table(0)
+        gather(v2_s, tab_s, idx2, 0, S)
+        nc.sync.dma_start(v2_s_last[0:100, :].bitcast(I32), v2_s[4:104, :].bitcast(I32))
+        gather(v_s, tab_s, idx, 0, S)
+        gather(v2_w[0], tab_w[0], idx2, 0, S)
+        gather(v_w[0], tab_w[0], idx, 0, S)
+        prepare_wa(0, 0)
+        prepare_wa(0, 1)
+        nc.sync.dma_start(wb_raw[:].bitcast(I32), wb_words.rearrange("a p c -> p a c").bitcast(I32))
+        for q in range(4):
+            nc.sync.dma_start(
+                wb_s_raw[32 * q : 32 * q + 4, :, :].bitcast(I32),
+                wb_scales[:, 4 * q : 4 * q + 4, :].rearrange("a r c -> r a c").bitcast(I32),
+            )
+        deal_wb(0)
+        deal_wb(1)
+        prepare_wa(1, 0)
+        prepare_wa(1, 1)
+        load_table(1)
+        gather(v2_w[1], tab_w[1], idx2, 0, S // 2)
+        gather(v_w[1], tab_w[1], idx, 0, S // 2)
+        load_load(0, 0)
+        hidden(0, 0)
+        load_load(0, 1)
+        hidden(0, 1)
+        gather(v2_w[1], tab_w[1], idx2, S // 2, S // 2)
+        gather(v_w[1], tab_w[1], idx, S // 2, S // 2)
+        prepare_wc(0, 0)
+        prepare_wc(1, 0)
+        nc.sync.dma_start(wgo_sb[:], wgo)
+        load_load(1, 0)
+        load_load(1, 1)
+        score(0, 0)
+        prepare_wc(0, 1)
+        prepare_wc(1, 1)
+        hidden(1, 0)
+        hidden(1, 1)
+        score(0, 1)
+        load_load(2, 0)
+        load_load(2, 1)
+        hidden(2, 0)
+        score(1, 0)
+        hidden(2, 1)
+        score(1, 1)
+        score(2, 0)
+        score(2, 1)

@@ -19,243 +19,253 @@ ALU = mybir.AluOpType
 P = 128
 PACK = 4
 PASS = P * PACK
-BANK = 512
+K_PASSES = K // PASS
+R_GROUPS = H // PASS
+PAGES = N // P
+QUADRANTS = 4
 LANES = 16
-CHUNKS = ((0, 256), (256, 256), (512, 512))
-HALF = N // 2
+BANK = 512
+CHUNK = BANK // 2
+CHUNKS = S // CHUNK
+WC_HALF = N // 2
 
 
 def tile_list_handover_row_scores_kernel(
     tc, tab_words, tab_scales, wa, wb_words, wb_scales, load, gain, wc, d, wgo, offs, offs2, offs3, out
 ):
     nc = tc.nc
-    KP, RP = K // PASS, H // PASS
 
     with ExitStack() as ctx:
         keep = ctx.enter_context(tc.tile_pool(name="keep", bufs=1))
-        raw = ctx.enter_context(tc.tile_pool(name="raw", bufs=4))
-        ring2 = ctx.enter_context(tc.tile_pool(name="ring2", bufs=2))
-        sums = ctx.enter_context(tc.tile_pool(name="sums", bufs=6))
+        large = ctx.enter_context(tc.tile_pool(name="large", bufs=2))
+        stage = ctx.enter_context(tc.tile_pool(name="stage", bufs=3))
         scores = ctx.enter_context(tc.tile_pool(name="scores", bufs=4))
-        psum1 = ctx.enter_context(tc.psum_pool(name="psum1", bufs=6))
-        psum2 = ctx.enter_context(tc.psum_pool(name="psum2", bufs=2))
+        psum_b = ctx.enter_context(tc.psum_pool(name="psum_b", bufs=6))
+        psum_z = ctx.enter_context(tc.psum_pool(name="psum_z", bufs=2))
 
         def held(name, shape, dtype):
             return keep.tile(shape, dtype, name=name, align_bytes=64)
 
-        lists = []
-        for name, src in (("idx", offs), ("idx2", offs2), ("idx3", offs3)):
+        def load_list(name, source):
             tile = held(name, [P, S // LANES], U16)
-            nc.sync.dma_start(tile[:], src)
-            lists.append(tile)
-        idx, idx2, idx3 = lists
-        gain_sb = held("gain_sb", [P, RP, PACK], F32)
-        nc.sync.dma_start(gain_sb[:], gain.rearrange("(g p t) -> p g t", g=RP, t=PACK))
-        d_sb = held("d_sb", [P, N // P], F32)
-        with nc.allow_non_contiguous_dma(reason="one bias value a partition"):
-            nc.sync.dma_start(d_sb[:], d.rearrange("(i p) -> p i", p=P))
+            nc.sync.dma_start(tile[:], source)
+            return tile
 
-        tab_s = held("tab_s", [P, T], U8)
-        nc.vector.memset(tab_s[:].bitcast(I32), 0)
-        for q in range(4):
-            nc.scalar.dma_start(
-                tab_s[32 * q : 32 * q + 4 * KP, :].bitcast(I32), tab_scales[:, 4 * q : 4 * q + 4, :].bitcast(I32)
-            )
-        wb_s_raw = held("wb_s_raw", [P, KP, H], U8)
-        nc.gpsimd.memset(wb_s_raw[:].bitcast(I32), 0)
-        v2_s_last = held("v2_s_last", [P, S], U8)
-        nc.gpsimd.memset(v2_s_last[:].bitcast(I32), 0)
-        pages = []
-        for i in range(N // P):
-            page = held("page%d" % i, [P, T2], F32)
-            (nc.vector, nc.gpsimd)[i % 2].memset(page[:], 0.0)
-            pages.append(page)
+        def gather(name, window, offsets, dtype):
+            picked = held(name, [P, S], dtype)
+            nc.vector.tensor_copy(picked[:], window[:].indirect(offsets[:]))
+            return picked
 
-        tab_w = [held("tab_w%d" % a, [P, T], U32) for a in range(KP)]
-        v_w = [held("v_w%d" % a, [P, S], U32) for a in range(KP)]
-        v2_w = [held("v2_w%d" % a, [P, S], U32) for a in range(KP)]
-        v_s = held("v_s", [P, S], U8)
-        v2_s = held("v2_s", [P, S], U8)
+        def gather_words(a):
+            table = held("table%d" % a, [P, T], U32)
+            nc.sync.dma_start(table[:].bitcast(I32), tab_words[a].rearrange("p c i -> p (c i)").bitcast(I32))
+            return gather("v2_words%d" % a, table, idx2, U32), gather("v_words%d" % a, table, idx, U32)
 
-        def load_table(a):
-            nc.sync.dma_start(tab_w[a][:].bitcast(I32), tab_words[a].rearrange("p t i -> p (t i)").bitcast(I32))
+        def quantise(name, rounded, columns):
+            words = held(name + "_words", [P, columns], U32)
+            scales = held(name + "_scales", [P, columns], U8)
+            nc.vector.quantize_mx(words[:].bitcast(FP8X4), scales[:], rounded[:])
+            return words, scales
 
-        def gather(dst, window, offsets, j0, width):
-            nc.vector.tensor_copy(
-                dst[:, j0 : j0 + width], window[:].indirect(offsets[:, j0 // LANES : (j0 + width) // LANES])
+        def weave(woven, rows):
+            return (
+                woven[:].rearrange("p (c e t) -> p c t e", e=PACK, t=PACK),
+                rows.rearrange("p t (c e) -> p c t e", e=PACK),
             )
 
-        wa_w, wa_s = {}, {}
+        wa_mx = {}
 
-        def prepare_wa(a, g):
-            rows = raw.tile([P, PACK, PASS], F32, name="rows")
-            nc.sync.dma_start(
-                rows[:], wa[a * PASS : (a + 1) * PASS, g * PASS : (g + 1) * PASS].rearrange("(p i) c -> p i c", i=PACK)
-            )
-            rounded = ring2.tile([P, PASS * PACK], BF16, name="wa_rounded", align_bytes=64)
-            nc.scalar.copy(
-                rounded[:].rearrange("p (t m i) -> p m i t", t=PACK, i=PACK),
-                rows[:].rearrange("p i (m t) -> p m i t", t=PACK),
-            )
-            wa_w[a, g] = held("wa_w%d%d" % (a, g), [P, PASS], U32)
-            wa_s[a, g] = held("wa_s%d%d" % (a, g), [P, PASS], U8)
-            nc.vector.quantize_mx(wa_w[a, g][:].bitcast(FP8X4), wa_s[a, g][:], rounded[:])
+        def prepare_wa(a):
+            rows = large.tile([P, PACK, H], F32, name="large")
+            nc.sync.dma_start(rows[:], wa[a * PASS : (a + 1) * PASS, :].rearrange("(p i) c -> p i c", i=PACK))
+            for g in range(R_GROUPS):
+                rounded = stage.tile([P, PASS * PACK], BF16, name="w_rounded", align_bytes=64)
+                nc.scalar.copy(
+                    rounded[:].rearrange("p (t m i) -> p m i t", t=PACK, i=PACK),
+                    rows[:, :, g * PASS : (g + 1) * PASS].rearrange("p i (m t) -> p m i t", t=PACK),
+                )
+                wa_mx[a, g] = quantise("wa%d%d" % (a, g), rounded, PASS)
 
-        wb_raw = held("wb_raw", [P, KP, 2 * H], U8)
-        wb_w, wb_s = {}, {}
+        wc_mx = {}
 
-        def deal_wb(g):
-            wb_w[g] = held("wb_w%d" % g, [P, KP, 2 * PASS], U8)
-            wb_s[g] = held("wb_s%d" % g, [P, KP, PASS], U8)
-            nc.vector.tensor_copy(
-                wb_w[g][:].bitcast(U16).rearrange("p a (t m) -> p a m t", t=PACK),
-                wb_raw[:].bitcast(U16)[:, :, g * PASS : (g + 1) * PASS].rearrange("p a (m t) -> p a m t", t=PACK),
-            )
-            nc.vector.tensor_copy(
-                wb_s[g][:].rearrange("p a (t m) -> p a m t", t=PACK),
-                wb_s_raw[:, :, g * PASS : (g + 1) * PASS].rearrange("p a (m t) -> p a m t", t=PACK),
-            )
+        def prepare_wc(half):
+            cols = slice(half * WC_HALF, (half + 1) * WC_HALF)
+            for g in range(R_GROUPS):
+                rows = held("wc_rows%d%d" % (g, half), [P, PACK, WC_HALF], F32)
+                nc.sync.dma_start(rows[:], wc[g * PASS : (g + 1) * PASS, cols].rearrange("(p t) n -> p t n", t=PACK))
+                rounded = stage.tile([P, WC_HALF * PACK], BF16, name="w_rounded", align_bytes=64)
+                nc.scalar.copy(*weave(rounded, rows[:]))
+                wc_mx[g, half] = quantise("wc%d%d" % (g, half), rounded, WC_HALF)
 
-        load_sb = {}
+        load_rows = {}
 
-        def load_load(c, g):
-            j0, width = CHUNKS[c]
-            if width == BANK:
-                tile = raw.tile([P, PACK, width], F32, name="rows")
-            else:
-                tile = held("load%d%d" % (c, g), [P, PACK, width], F32)
-            nc.sync.dma_start(
-                tile[:], load[g * PASS : (g + 1) * PASS, j0 : j0 + width].rearrange("(p t) j -> p t j", t=PACK)
-            )
-            load_sb[c, g] = tile
+        def bring_load(first_chunk, tiles):
+            for g, tile in enumerate(tiles):
+                width = tile.shape[2]
+                cols = slice(first_chunk * CHUNK, first_chunk * CHUNK + width)
+                nc.sync.dma_start(tile, load[g * PASS : (g + 1) * PASS, cols].rearrange("(p t) j -> p t j", t=PACK))
+                for c in range(width // CHUNK):
+                    load_rows[first_chunk + c, g] = tile[:, :, c * CHUNK : (c + 1) * CHUNK]
 
-        wc_w, wc_s = {}, {}
+        def bring_load_chunk(c):
+            bring_load(c, [held("load%d%d" % (c, g), [P, PACK, CHUNK], F32)[:] for g in range(R_GROUPS)])
 
-        def prepare_wc(g, half):
-            rows = ring2.tile([P, PACK, HALF], F32, name="wc_rows")
-            nc.sync.dma_start(
-                rows[:], wc[g * PASS : (g + 1) * PASS, half * HALF : (half + 1) * HALF].rearrange("(p t) n -> p t n", t=PACK)
-            )
-            rounded = ring2.tile([P, HALF * PACK], BF16, name="wc_rounded", align_bytes=64)
-            nc.scalar.copy(
-                rounded[:].rearrange("p (c e t) -> p c t e", e=PACK, t=PACK),
-                rows[:].rearrange("p t (c e) -> p c t e", e=PACK),
-            )
-            wc_w[g, half] = held("wc_w%d%d" % (g, half), [P, HALF], U32)
-            wc_s[g, half] = held("wc_s%d%d" % (g, half), [P, HALF], U8)
-            nc.vector.quantize_mx(wc_w[g, half][:].bitcast(FP8X4), wc_s[g, half][:], rounded[:])
-
-        h_w, h_s = {}, {}
+        h_mx = {}
 
         def hidden(c, g):
-            j0, width = CHUNKS[c]
-            cols = slice(j0, j0 + width)
-            per_bank = BANK // width
-            h_rows = ring2.tile([P, PACK, width], BF16, name="h_rows", align_bytes=64)
-            for t0 in range(0, PACK, per_bank):
-                b = psum1.tile([P, per_bank, width], F32, name="b")
+            cols = slice(c * CHUNK, (c + 1) * CHUNK)
+            x = load_rows[c, g]
+            for pair in range(0, PACK, 2):
+                b = psum_b.tile([P, 2, CHUNK], F32, name="b")
                 passes = []
-                for a in range(KP):
-                    for t in range(t0, t0 + per_bank):
-                        m = slice(t * P, (t + 1) * P)
+                for a in range(K_PASSES):
+                    for t in (pair, pair + 1):
                         passes.append((
-                            t, wb_w[g][:, a, 2 * t * P : 2 * (t + 1) * P].bitcast(FP4X4), wb_s[g][:, a, m],
-                            v2_w[a][:, cols], (v2_s, v2_s_last)[a][:, cols],
+                            t,
+                            wb_dealt[:, a * R_GROUPS + g, 2 * t * P : 2 * (t + 1) * P].bitcast(FP4X4),
+                            wb_scales_dealt[:, a * R_GROUPS + g, t * P : (t + 1) * P],
+                            v2_words[a][:, cols],
+                            v2_scales[a][:, cols],
                         ))
-                    for t in range(t0, t0 + per_bank):
-                        m = slice(t * P, (t + 1) * P)
+                    for t in (pair, pair + 1):
+                        words, scales = wa_mx[a, g]
                         passes.append((
-                            t, wa_w[a, g][:, m].bitcast(FP8X4), wa_s[a, g][:, m], v_w[a][:, cols], v_s[4 * a :, cols],
+                            t,
+                            words[:, t * P : (t + 1) * P].bitcast(FP8X4),
+                            scales[:, t * P : (t + 1) * P],
+                            v_words[a][:, cols],
+                            v_scales[PACK * a :, cols],
                         ))
-                for n, (t, w, w_scale, v, v_scale) in enumerate(passes):
+                for n, (t, weight, weight_scale, picked, picked_scale) in enumerate(passes):
                     nc.tensor.matmul_mx(
-                        b[:, t - t0, :], lhsT=w, lhsT_scale=w_scale, rhs=v.bitcast(FP8X4), rhs_scale=v_scale,
+                        b[:, t - pair, :], lhsT=weight, lhsT_scale=weight_scale,
+                        rhs=picked.bitcast(FP8X4), rhs_scale=picked_scale,
                         start=(n == 0), stop=(n == len(passes) - 1),
                     )
-                x = sums.tile([P, per_bank, width], F32, name="x")
-                nc.vector.tensor_tensor(x[:], b[:], load_sb[c, g][:, t0 : t0 + per_bank, :], ALU.add)
-                nc.scalar.activation(x[:], x[:], ACT.Tanh)
-                for t in range(t0, t0 + per_bank):
-                    nc.scalar.activation(h_rows[:, t, :], x[:, t - t0, :], ACT.Copy, scale=gain_sb[:, g, t : t + 1])
-            h_woven = ring2.tile([P, width * PACK], BF16, name="h_woven", align_bytes=64)
-            nc.scalar.copy(
-                h_woven[:].rearrange("p (c e t) -> p c t e", e=PACK, t=PACK),
-                h_rows[:].rearrange("p t (c e) -> p c t e", e=PACK),
-            )
-            h_w[c, g] = held("h_w%d%d" % (c, g), [P, width], U32)
-            h_s[c, g] = held("h_s%d%d" % (c, g), [P, width], U8)
-            nc.vector.quantize_mx(h_w[c, g][:].bitcast(FP8X4), h_s[c, g][:], h_woven[:])
+                nc.vector.tensor_tensor(x[:, pair : pair + 2, :], b[:], x[:, pair : pair + 2, :], ALU.add)
 
-        wgo_sb = held("wgo_sb", [P, S], F32)
+            h_woven = stage.tile([P, CHUNK * PACK], BF16, name="h_woven", align_bytes=64)
+            if c == 0 or (g == 1 and c < CHUNKS - 1):
+                tanh_woven = stage.tile([P, CHUNK * PACK], F32, name="tanh_woven", bufs=2)
+                nc.scalar.activation(*weave(tanh_woven, x), ACT.Tanh)
+                nc.vector.tensor_tensor(
+                    h_woven[:].rearrange("p (j t) -> p j t", t=PACK),
+                    tanh_woven[:].rearrange("p (j t) -> p j t", t=PACK),
+                    gain_sb[:, g : g + 1, :].to_broadcast([P, CHUNK, PACK]),
+                    ALU.mult,
+                )
+            else:
+                h_rows = stage.tile([P, PACK, CHUNK], BF16, name="h_rows")
+                nc.scalar.activation(x, x, ACT.Tanh)
+                for t in range(PACK):
+                    nc.scalar.activation(h_rows[:, t, :], x[:, t, :], ACT.Copy, scale=gain_sb[:, g, t : t + 1])
+                nc.scalar.copy(*weave(h_woven, h_rows[:]))
+            h_mx[c, g] = quantise("h%d%d" % (c, g), h_woven, CHUNK)
 
-        def score(c, half):
-            j0, width = CHUNKS[c]
-            per_bank = BANK // width
-            for i0 in range(2 * half, 2 * half + 2, per_bank):
-                z = psum2.tile([P, per_bank, width], F32, name="z")
-                y = scores.tile([P, per_bank, width], F32, name="y")
-                for i in range(i0, i0 + per_bank):
-                    m = slice((i % 2) * P, (i % 2 + 1) * P)
-                    for g in range(RP):
-                        nc.tensor.matmul_mx(
-                            z[:, i - i0, :], lhsT=wc_w[g, half][:, m].bitcast(FP8X4), lhsT_scale=wc_s[g, half][:, m],
-                            rhs=h_w[c, g][:].bitcast(FP8X4), rhs_scale=h_s[c, g][:],
-                            start=(g == 0), stop=(g == RP - 1),
-                        )
-                for i in range(i0, i0 + per_bank):
-                    nc.scalar.activation(y[:, i - i0, :], z[:, i - i0, :], ACT.Abs, bias=d_sb[:, i : i + 1])
-                nc.scalar.activation(y[:], y[:], ACT.Exp, scale=-1.0)
-                for i in range(i0, i0 + per_bank):
-                    nc.vector.tensor_tensor(
-                        pages[i][:].indirect(idx3[:, j0 // LANES : (j0 + width) // LANES]),
-                        y[:, i - i0, :], wgo_sb[:, j0 : j0 + width], ALU.mult,
+        def score(parts):
+            z = psum_z.tile([P, BANK], F32, name="z")
+            y = scores.tile([P, BANK], F32, name="y")
+            for n, (i, c) in enumerate(parts):
+                m = slice((i % 2) * P, (i % 2 + 1) * P)
+                for g in range(R_GROUPS):
+                    wc_words, wc_scales = wc_mx[g, i // 2]
+                    h_words, h_scales = h_mx[c, g]
+                    nc.tensor.matmul_mx(
+                        z[:, n * CHUNK : (n + 1) * CHUNK], lhsT=wc_words[:, m].bitcast(FP8X4), lhsT_scale=wc_scales[:, m],
+                        rhs=h_words[:].bitcast(FP8X4), rhs_scale=h_scales[:],
+                        start=(g == 0), stop=(g == R_GROUPS - 1),
                     )
-                    if c == len(CHUNKS) - 1:
-                        nc.sync.dma_start(out[i * P : (i + 1) * P, :], pages[i][:])
+            (i0, c0), (i1, c1) = parts
+            if i0 == i1:
+                runs = [(i0, c0, slice(0, BANK))]
+            else:
+                runs = [(i0, c0, slice(0, CHUNK)), (i1, c1, slice(CHUNK, BANK))]
+            for i, c, cols in runs:
+                nc.scalar.activation(y[:, cols], z[:, cols], ACT.Abs, bias=d_sb[:, i : i + 1])
+            nc.scalar.activation(y[:], y[:], ACT.Exp, scale=-1.0)
+            for i, c, cols in runs:
+                j0, j1 = c * CHUNK, c * CHUNK + cols.stop - cols.start
+                nc.vector.tensor_tensor(
+                    pages[i][:].indirect(idx3[:, j0 // LANES : j1 // LANES]), y[:, cols], wgo_sb[:, j0:j1], ALU.mult
+                )
+                if j1 == S:
+                    nc.sync.dma_start(out[i * P : (i + 1) * P, :], pages[i][:])
 
-        load_table(0)
-        gather(v2_s, tab_s, idx2, 0, S)
-        nc.sync.dma_start(v2_s_last[0:100, :].bitcast(I32), v2_s[4:104, :].bitcast(I32))
-        gather(v_s, tab_s, idx, 0, S)
-        gather(v2_w[0], tab_w[0], idx2, 0, S)
-        gather(v_w[0], tab_w[0], idx, 0, S)
-        prepare_wa(0, 0)
-        prepare_wa(0, 1)
-        nc.sync.dma_start(wb_raw[:].bitcast(I32), wb_words.rearrange("a p c -> p a c").bitcast(I32))
-        for q in range(4):
+        idx2 = load_list("idx2", offs2)
+        idx = load_list("idx", offs)
+        table_scales = held("table_scales", [P, T], U8)
+        nc.vector.memset(table_scales[:].bitcast(I32), 0)
+        wb_scales_raw = held("wb_scales_raw", [P, K_PASSES, H], U8)
+        nc.gpsimd.memset(wb_scales_raw[:].bitcast(I32), 0)
+        v2_scales_last = held("v2_scales_last", [P, S], U8)
+        nc.gpsimd.memset(v2_scales_last[:].bitcast(I32), 0)
+        idx3 = load_list("idx3", offs3)
+        gain_sb = held("gain_sb", [P, R_GROUPS, PACK], F32)
+        nc.sync.dma_start(gain_sb[:], gain.rearrange("(g p t) -> p g t", g=R_GROUPS, t=PACK))
+
+        v2_words, v_words = [None] * K_PASSES, [None] * K_PASSES
+        v2_words[0], v_words[0] = gather_words(0)
+        prepare_wa(0)
+        wb_raw = held("wb_raw", [P, K_PASSES, 2 * H], U8)
+        for a in range(K_PASSES):
+            nc.sync.dma_start(wb_raw[:, a, :].bitcast(I32), wb_words[a].bitcast(I32))
+
+        for q in range(QUADRANTS):
             nc.sync.dma_start(
-                wb_s_raw[32 * q : 32 * q + 4, :, :].bitcast(I32),
-                wb_scales[:, 4 * q : 4 * q + 4, :].rearrange("a r c -> r a c").bitcast(I32),
+                table_scales[32 * q : 32 * q + PACK * K_PASSES, :].bitcast(I32),
+                tab_scales[:, PACK * q : PACK * (q + 1), :].bitcast(I32),
             )
-        deal_wb(0)
-        deal_wb(1)
-        prepare_wa(1, 0)
-        prepare_wa(1, 1)
-        load_table(1)
-        gather(v2_w[1], tab_w[1], idx2, 0, S // 2)
-        gather(v_w[1], tab_w[1], idx, 0, S // 2)
-        load_load(0, 0)
-        hidden(0, 0)
-        load_load(0, 1)
-        hidden(0, 1)
-        gather(v2_w[1], tab_w[1], idx2, S // 2, S // 2)
-        gather(v_w[1], tab_w[1], idx, S // 2, S // 2)
-        prepare_wc(0, 0)
-        prepare_wc(1, 0)
-        nc.sync.dma_start(wgo_sb[:], wgo)
-        load_load(1, 0)
-        load_load(1, 1)
-        score(0, 0)
-        prepare_wc(0, 1)
-        prepare_wc(1, 1)
-        hidden(1, 0)
-        hidden(1, 1)
-        score(0, 1)
-        load_load(2, 0)
-        load_load(2, 1)
-        hidden(2, 0)
-        score(1, 0)
-        hidden(2, 1)
-        score(1, 1)
-        score(2, 0)
-        score(2, 1)
+        v2_scales_both = gather("v2_scales_both", table_scales, idx2, U8)
+        moved = 32 * (QUADRANTS - 1) + PACK
+        nc.sync.dma_start(v2_scales_last[0:moved, :].bitcast(I32), v2_scales_both[PACK : PACK + moved, :].bitcast(I32))
+        v2_scales = (v2_scales_both, v2_scales_last)
+        v_scales = gather("v_scales", table_scales, idx, U8)
+
+        prepare_wa(1)
+        for s in range(PACK):
+            nc.sync.dma_start(
+                wb_scales_raw[s : P : 32, :, :].bitcast(I32),
+                wb_scales[:, s : PACK * QUADRANTS : PACK, :].rearrange("a q c -> q a c").bitcast(I32),
+            )
+        wb_dealt = held("wb_dealt", [P, K_PASSES * R_GROUPS, 2 * PASS], U8)
+        nc.vector.tensor_copy(
+            wb_dealt[:].bitcast(U16).rearrange("p n (t m) -> p n t m", t=PACK),
+            wb_raw[:].bitcast(U16).rearrange("p a (g m t) -> p (a g) t m", g=R_GROUPS, t=PACK),
+        )
+        wb_scales_dealt = held("wb_scales_dealt", [P, K_PASSES * R_GROUPS, PASS], U8)
+        nc.vector.tensor_copy(
+            wb_scales_dealt[:].rearrange("p n (t m) -> p n t m", t=PACK),
+            wb_scales_raw[:].rearrange("p a (g m t) -> p (a g) t m", g=R_GROUPS, t=PACK),
+        )
+        v2_words[1], v_words[1] = gather_words(1)
+
+        bring_load_chunk(0)
+        for g in range(R_GROUPS):
+            hidden(0, g)
+        prepare_wc(0)
+        d_sb = held("d_sb", [P, PAGES], F32)
+        with nc.allow_non_contiguous_dma(reason="one bias value a partition and page"):
+            nc.sync.dma_start(d_sb[:], d.rearrange("(i p) -> p i", p=P))
+        wgo_sb = held("wgo_sb", [P, S], F32)
+        nc.sync.dma_start(wgo_sb[:, : S // 2], wgo[:, : S // 2])
+        bring_load_chunk(1)
+        prepare_wc(1)
+        late_load = large.tile([P, R_GROUPS, PACK, S // 2], F32, name="large")
+        bring_load(CHUNKS // 2, [late_load[:, g] for g in range(R_GROUPS)])
+        nc.sync.dma_start(wgo_sb[:, S // 2 :], wgo[:, S // 2 :])
+
+        pages = [held("page%d" % i, [P, T2], F32) for i in range(PAGES)]
+        for page in pages[:-1]:
+            nc.vector.memset(page[:], 0.0)
+        nc.gpsimd.memset(pages[-1][:], 0.0)
+
+        last = CHUNKS - 1
+        for c in range(last):
+            for g in range(R_GROUPS):
+                hidden(c + 1, g)
+            score([(0, c), (1, c)])
+            if c < last - 1:
+                score([(2, c), (3, c)])
+        score([(0, last), (1, last)])
+        for i in (2, 3):
+            score([(i, last - 1), (i, last)])

@@ -75,26 +75,24 @@ def tile_list_handover_row_scores_kernel(
 
         wa_mx = {}
 
-        def prepare_wa(a):
-            rows = large.tile([P, PACK, H], F32, name="large")
-            nc.sync.dma_start(rows[:], wa[a * PASS : (a + 1) * PASS, :].rearrange("(p i) c -> p i c", i=PACK))
-            for g in range(R_GROUPS):
-                rounded = stage.tile([P, PASS * PACK], BF16, name="w_rounded", align_bytes=64)
-                nc.scalar.copy(
-                    rounded[:].rearrange("p (t m i) -> p m i t", t=PACK, i=PACK),
-                    rows[:, :, g * PASS : (g + 1) * PASS].rearrange("p i (m t) -> p m i t", t=PACK),
-                )
-                wa_mx[a, g] = quantise("wa%d%d" % (a, g), rounded, PASS)
+        def prepare_wa(a, g, rows):
+            rounded = stage.tile([P, PASS * PACK], BF16, name="w_rounded", align_bytes=64)
+            nc.scalar.copy(
+                rounded[:].rearrange("p (t m i) -> p m i t", t=PACK, i=PACK),
+                rows.rearrange("p i (m t) -> p m i t", t=PACK),
+            )
+            wa_mx[a, g] = quantise("wa%d%d" % (a, g), rounded, PASS)
 
         wc_mx = {}
 
         def prepare_wc(half):
-            cols = slice(half * WC_HALF, (half + 1) * WC_HALF)
             for g in range(R_GROUPS):
-                rows = held("wc_rows%d%d" % (g, half), [P, PACK, WC_HALF], F32)
-                nc.sync.dma_start(rows[:], wc[g * PASS : (g + 1) * PASS, cols].rearrange("(p t) n -> p t n", t=PACK))
                 rounded = stage.tile([P, WC_HALF * PACK], BF16, name="w_rounded", align_bytes=64)
-                nc.scalar.copy(*weave(rounded, rows[:]))
+                nc.gpsimd.tensor_scalar(
+                    rounded[:].rearrange("p (n t) -> p n t", t=PACK),
+                    wc_rows[:, g, :, half * WC_HALF : (half + 1) * WC_HALF].rearrange("p t n -> p n t"),
+                    1.0, 0.0, ALU.mult, ALU.add,
+                )
                 wc_mx[g, half] = quantise("wc%d%d" % (g, half), rounded, WC_HALF)
 
         load_rows = {}
@@ -145,7 +143,7 @@ def tile_list_handover_row_scores_kernel(
                 nc.vector.tensor_tensor(x[:, pair : pair + 2, :], b[:], x[:, pair : pair + 2, :], ALU.add)
 
             h_woven = stage.tile([P, CHUNK * PACK], BF16, name="h_woven", align_bytes=64)
-            if c == 0 or (g == 1 and c < CHUNKS - 1):
+            if g == 1 and c < CHUNKS - 1:
                 tanh_woven = stage.tile([P, CHUNK * PACK], F32, name="tanh_woven", bufs=2)
                 nc.scalar.activation(*weave(tanh_woven, x), ACT.Tanh)
                 nc.vector.tensor_tensor(
@@ -205,10 +203,11 @@ def tile_list_handover_row_scores_kernel(
 
         v2_words, v_words = [None] * K_PASSES, [None] * K_PASSES
         v2_words[0], v_words[0] = gather_words(0)
-        prepare_wa(0)
         wb_raw = held("wb_raw", [P, K_PASSES, 2 * H], U8)
         for a in range(K_PASSES):
             nc.sync.dma_start(wb_raw[:, a, :].bitcast(I32), wb_words[a].bitcast(I32))
+        wgo_sb = held("wgo_sb", [P, S], F32)
+        nc.sync.dma_start(wgo_sb[:, : S // 2], wgo[:, : S // 2])
 
         for q in range(QUADRANTS):
             nc.sync.dma_start(
@@ -221,7 +220,10 @@ def tile_list_handover_row_scores_kernel(
         v2_scales = (v2_scales_both, v2_scales_last)
         v_scales = gather("v_scales", table_scales, idx, U8)
 
-        prepare_wa(1)
+        wa_first = large.tile([P, PACK, H], F32, name="large")
+        nc.sync.dma_start(wa_first[:], wa[:PASS, :].rearrange("(p i) c -> p i c", i=PACK))
+        for g in range(R_GROUPS):
+            prepare_wa(0, g, wa_first[:, :, g * PASS : (g + 1) * PASS])
         for s in range(PACK):
             nc.sync.dma_start(
                 wb_scales_raw[s : P : 32, :, :].bitcast(I32),
@@ -238,20 +240,27 @@ def tile_list_handover_row_scores_kernel(
             wb_scales_raw[:].rearrange("p a (g m t) -> p (a g) t m", g=R_GROUPS, t=PACK),
         )
         v2_words[1], v_words[1] = gather_words(1)
+        wa_second = large.tile([P, R_GROUPS, PACK, PASS], F32, name="large")
+        for g in range(R_GROUPS):
+            nc.sync.dma_start(
+                wa_second[:, g], wa[PASS:, g * PASS : (g + 1) * PASS].rearrange("(p i) c -> p i c", i=PACK)
+            )
+            prepare_wa(1, g, wa_second[:, g])
 
         bring_load_chunk(0)
         for g in range(R_GROUPS):
             hidden(0, g)
+        bring_load_chunk(1)
+        wc_rows = held("wc_rows", [P, R_GROUPS, PACK, N], F32)
+        for g in range(R_GROUPS):
+            nc.sync.dma_start(wc_rows[:, g], wc[g * PASS : (g + 1) * PASS, :].rearrange("(p t) n -> p t n", t=PACK))
         prepare_wc(0)
         d_sb = held("d_sb", [P, PAGES], F32)
         with nc.allow_non_contiguous_dma(reason="one bias value a partition and page"):
             nc.sync.dma_start(d_sb[:], d.rearrange("(i p) -> p i", p=P))
-        wgo_sb = held("wgo_sb", [P, S], F32)
-        nc.sync.dma_start(wgo_sb[:, : S // 2], wgo[:, : S // 2])
-        bring_load_chunk(1)
-        prepare_wc(1)
         late_load = large.tile([P, R_GROUPS, PACK, S // 2], F32, name="large")
         bring_load(CHUNKS // 2, [late_load[:, g] for g in range(R_GROUPS)])
+        prepare_wc(1)
         nc.sync.dma_start(wgo_sb[:, S // 2 :], wgo[:, S // 2 :])
 
         pages = [held("page%d" % i, [P, T2], F32) for i in range(PAGES)]

@@ -88,11 +88,8 @@ def tile_list_handover_row_scores_kernel(
         def prepare_wc(half):
             for g in range(R_GROUPS):
                 rounded = stage.tile([P, WC_HALF * PACK], BF16, name="w_rounded", align_bytes=64)
-                nc.gpsimd.tensor_scalar(
-                    rounded[:].rearrange("p (n t) -> p n t", t=PACK),
-                    wc_rows[:, g, :, half * WC_HALF : (half + 1) * WC_HALF].rearrange("p t n -> p n t"),
-                    1.0, 0.0, ALU.mult, ALU.add,
-                )
+                copy = nc.scalar.copy if half == 0 else nc.vector.tensor_copy
+                copy(*weave(rounded, wc_rows[:, g, :, half * WC_HALF : (half + 1) * WC_HALF]))
                 wc_mx[g, half] = quantise("wc%d%d" % (g, half), rounded, WC_HALF)
 
         load_rows = {}

from contextlib import ExitStack

import concourse.mybir as mybir

K, T, S, H, N, T2 = 1024, 4096, 1024, 1024, 512, 2048
FLOPS = 2 * S * H * (2 * K + N)

F32 = mybir.dt.float32
BF16 = mybir.dt.bfloat16
I32 = mybir.dt.int32
U32 = mybir.dt.uint32
U16 = mybir.dt.uint16
U8 = mybir.dt.uint8
FP8X4 = mybir.dt.float8_e4m3fn_x4
FP4X4 = mybir.dt.float4_e2m1fn_x4
ACT = mybir.ActivationFunctionType
ALU = mybir.AluOpType

P = 128
PACK = 4
PASS = P * PACK
K_PASSES = K // PASS
R_GROUPS = H // PASS
PAGES = N // P
QUADRANTS = 4
LANES = 16
BANK = 512
CHUNK = BANK // 2
CHUNKS = S // CHUNK
WC_HALF = N // 2


def tile_list_handover_row_scores_kernel(
    tc, tab_words, tab_scales, wa, wb_words, wb_scales, load, gain, wc, d, wgo, offs, offs2, offs3, out
):
    nc = tc.nc

    with ExitStack() as ctx:
        keep = ctx.enter_context(tc.tile_pool(name="keep", bufs=1))
        large = ctx.enter_context(tc.tile_pool(name="large", bufs=2))
        stage = ctx.enter_context(tc.tile_pool(name="stage", bufs=3))
        scores = ctx.enter_context(tc.tile_pool(name="scores", bufs=4))
        psum_b = ctx.enter_context(tc.psum_pool(name="psum_b", bufs=6))
        psum_z = ctx.enter_context(tc.psum_pool(name="psum_z", bufs=2))

        def held(name, shape, dtype):
            return keep.tile(shape, dtype, name=name, align_bytes=64)

        def load_list(name, source):
            tile = held(name, [P, S // LANES], U16)
            nc.sync.dma_start(tile[:], source)
            return tile

        def gather(name, window, offsets, dtype):
            picked = held(name, [P, S], dtype)
            nc.vector.tensor_copy(picked[:], window[:].indirect(offsets[:]))
            return picked

        def gather_words(a):
            table = held("table%d" % a, [P, T], U32)
            nc.sync.dma_start(table[:].bitcast(I32), tab_words[a].rearrange("p c i -> p (c i)").bitcast(I32))
            return gather("v2_words%d" % a, table, idx2, U32), gather("v_words%d" % a, table, idx, U32)

        def quantise(name, rounded, columns):
            words = held(name + "_words", [P, columns], U32)
            scales = held(name + "_scales", [P, columns], U8)
            nc.vector.quantize_mx(words[:].bitcast(FP8X4), scales[:], rounded[:])
            return words, scales

        def weave(woven, rows):
            return (
                woven[:].rearrange("p (c e t) -> p c t e", e=PACK, t=PACK),
                rows.rearrange("p t (c e) -> p c t e", e=PACK),
            )

        wa_mx = {}

        def prepare_wa(a, g, rows):
            rounded = stage.tile([P, PASS * PACK], BF16, name="w_rounded", align_bytes=64)
            nc.scalar.copy(
                rounded[:].rearrange("p (t m i) -> p m i t", t=PACK, i=PACK),
                rows.rearrange("p i (m t) -> p m i t", t=PACK),
            )
            wa_mx[a, g] = quantise("wa%d%d" % (a, g), rounded, PASS)

        wc_mx = {}

        def prepare_wc(half):
            for g in range(R_GROUPS):
                rounded = stage.tile([P, WC_HALF * PACK], BF16, name="w_rounded", align_bytes=64)
                copy = nc.scalar.copy if half == 0 else nc.vector.tensor_copy
                copy(*weave(rounded, wc_rows[:, g, :, half * WC_HALF : (half + 1) * WC_HALF]))
                wc_mx[g, half] = quantise("wc%d%d" % (g, half), rounded, WC_HALF)

        load_rows = {}

        def bring_load(first_chunk, tiles):
            for g, tile in enumerate(tiles):
                width = tile.shape[2]
                cols = slice(first_chunk * CHUNK, first_chunk * CHUNK + width)
                nc.sync.dma_start(tile, load[g * PASS : (g + 1) * PASS, cols].rearrange("(p t) j -> p t j", t=PACK))
                for c in range(width // CHUNK):
                    load_rows[first_chunk + c, g] = tile[:, :, c * CHUNK : (c + 1) * CHUNK]

        def bring_load_chunk(c):
            bring_load(c, [held("load%d%d" % (c, g), [P, PACK, CHUNK], F32)[:] for g in range(R_GROUPS)])

        h_mx = {}

        def hidden(c, g):
            cols = slice(c * CHUNK, (c + 1) * CHUNK)
            x = load_rows[c, g]
            for pair in range(0, PACK, 2):
                b = psum_b.tile([P, 2, CHUNK], F32, name="b")
                passes = []
                for a in range(K_PASSES):
                    for t in (pair, pair + 1):
                        passes.append((
                            t,
                            wb_dealt[:, a * R_GROUPS + g, 2 * t * P : 2 * (t + 1) * P].bitcast(FP4X4),
                            wb_scales_dealt[:, a * R_GROUPS + g, t * P : (t + 1) * P],
                            v2_words[a][:, cols],
                            v2_scales[a][:, cols],
                        ))
                    for t in (pair, pair + 1):
                        words, scales = wa_mx[a, g]
                        passes.append((
                            t,
                            words[:, t * P : (t + 1) * P].bitcast(FP8X4),
                            scales[:, t * P : (t + 1) * P],
                            v_words[a][:, cols],
                            v_scales[PACK * a :, cols],
                        ))
                for n, (t, weight, weight_scale, picked, picked_scale) in enumerate(passes):
                    nc.tensor.matmul_mx(
                        b[:, t - pair, :], lhsT=weight, lhsT_scale=weight_scale,
                        rhs=picked.bitcast(FP8X4), rhs_scale=picked_scale,
                        start=(n == 0), stop=(n == len(passes) - 1),
                    )
                nc.vector.tensor_tensor(x[:, pair : pair + 2, :], b[:], x[:, pair : pair + 2, :], ALU.add)

            h_woven = stage.tile([P, CHUNK * PACK], BF16, name="h_woven", align_bytes=64)
            if g == 1 and c < CHUNKS - 1:
                tanh_woven = stage.tile([P, CHUNK * PACK], F32, name="tanh_woven", bufs=2)
                nc.scalar.activation(*weave(tanh_woven, x), ACT.Tanh)
                nc.vector.tensor_tensor(
                    h_woven[:].rearrange("p (j t) -> p j t", t=PACK),
                    tanh_woven[:].rearrange("p (j t) -> p j t", t=PACK),
                    gain_sb[:, g : g + 1, :].to_broadcast([P, CHUNK, PACK]),
                    ALU.mult,
                )
            else:
                h_rows = stage.tile([P, PACK, CHUNK], BF16, name="h_rows")
                nc.scalar.activation(x, x, ACT.Tanh)
                for t in range(PACK):
                    nc.scalar.activation(h_rows[:, t, :], x[:, t, :], ACT.Copy, scale=gain_sb[:, g, t : t + 1])
                nc.scalar.copy(*weave(h_woven, h_rows[:]))
            h_mx[c, g] = quantise("h%d%d" % (c, g), h_woven, CHUNK)

        def score(parts):
            z = psum_z.tile([P, BANK], F32, name="z")
            y = scores.tile([P, BANK], F32, name="y")
            for n, (i, c) in enumerate(parts):
                m = slice((i % 2) * P, (i % 2 + 1) * P)
                for g in range(R_GROUPS):
                    wc_words, wc_scales = wc_mx[g, i // 2]
                    h_words, h_scales = h_mx[c, g]
                    nc.tensor.matmul_mx(
                        z[:, n * CHUNK : (n + 1) * CHUNK], lhsT=wc_words[:, m].bitcast(FP8X4), lhsT_scale=wc_scales[:, m],
                        rhs=h_words[:].bitcast(FP8X4), rhs_scale=h_scales[:],
                        start=(g == 0), stop=(g == R_GROUPS - 1),
                    )
            (i0, c0), (i1, c1) = parts
            if i0 == i1:
                runs = [(i0, c0, slice(0, BANK))]
            else:
                runs = [(i0, c0, slice(0, CHUNK)), (i1, c1, slice(CHUNK, BANK))]
            for i, c, cols in runs:
                nc.scalar.activation(y[:, cols], z[:, cols], ACT.Abs, bias=d_sb[:, i : i + 1])
            nc.scalar.activation(y[:], y[:], ACT.Exp, scale=-1.0)
            for i, c, cols in runs:
                j0, j1 = c * CHUNK, c * CHUNK + cols.stop - cols.start
                nc.vector.tensor_tensor(
                    pages[i][:].indirect(idx3[:, j0 // LANES : j1 // LANES]), y[:, cols], wgo_sb[:, j0:j1], ALU.mult
                )
                if j1 == S:
                    nc.sync.dma_start(out[i * P : (i + 1) * P, :], pages[i][:])

        idx2 = load_list("idx2", offs2)
        idx = load_list("idx", offs)
        table_scales = held("table_scales", [P, T], U8)
        nc.vector.memset(table_scales[:].bitcast(I32), 0)
        wb_scales_raw = held("wb_scales_raw", [P, K_PASSES, H], U8)
        nc.gpsimd.memset(wb_scales_raw[:].bitcast(I32), 0)
        v2_scales_last = held("v2_scales_last", [P, S], U8)
        nc.gpsimd.memset(v2_scales_last[:].bitcast(I32), 0)
        idx3 = load_list("idx3", offs3)
        gain_sb = held("gain_sb", [P, R_GROUPS, PACK], F32)
        nc.sync.dma_start(gain_sb[:], gain.rearrange("(g p t) -> p g t", g=R_GROUPS, t=PACK))

        v2_words, v_words = [None] * K_PASSES, [None] * K_PASSES
        v2_words[0], v_words[0] = gather_words(0)
        wb_raw = held("wb_raw", [P, K_PASSES, 2 * H], U8)
        for a in range(K_PASSES):
            nc.sync.dma_start(wb_raw[:, a, :].bitcast(I32), wb_words[a].bitcast(I32))
        wgo_sb = held("wgo_sb", [P, S], F32)
        nc.sync.dma_start(wgo_sb[:, : S // 2], wgo[:, : S // 2])

        for q in range(QUADRANTS):
            nc.sync.dma_start(
                table_scales[32 * q : 32 * q + PACK * K_PASSES, :].bitcast(I32),
                tab_scales[:, PACK * q : PACK * (q + 1), :].bitcast(I32),
            )
        v2_scales_both = gather("v2_scales_both", table_scales, idx2, U8)
        moved = 32 * (QUADRANTS - 1) + PACK
        nc.sync.dma_start(v2_scales_last[0:moved, :].bitcast(I32), v2_scales_both[PACK : PACK + moved, :].bitcast(I32))
        v2_scales = (v2_scales_both, v2_scales_last)
        v_scales = gather("v_scales", table_scales, idx, U8)

        wa_first = large.tile([P, PACK, H], F32, name="large")
        nc.sync.dma_start(wa_first[:], wa[:PASS, :].rearrange("(p i) c -> p i c", i=PACK))
        for g in range(R_GROUPS):
            prepare_wa(0, g, wa_first[:, :, g * PASS : (g + 1) * PASS])
        for s in range(PACK):
            nc.sync.dma_start(
                wb_scales_raw[s : P : 32, :, :].bitcast(I32),
                wb_scales[:, s : PACK * QUADRANTS : PACK, :].rearrange("a q c -> q a c").bitcast(I32),
            )
        wb_dealt = held("wb_dealt", [P, K_PASSES * R_GROUPS, 2 * PASS], U8)
        nc.vector.tensor_copy(
            wb_dealt[:].bitcast(U16).rearrange("p n (t m) -> p n t m", t=PACK),
            wb_raw[:].bitcast(U16).rearrange("p a (g m t) -> p (a g) t m", g=R_GROUPS, t=PACK),
        )
        wb_scales_dealt = held("wb_scales_dealt", [P, K_PASSES * R_GROUPS, PASS], U8)
        nc.vector.tensor_copy(
            wb_scales_dealt[:].rearrange("p n (t m) -> p n t m", t=PACK),
            wb_scales_raw[:].rearrange("p a (g m t) -> p (a g) t m", g=R_GROUPS, t=PACK),
        )
        v2_words[1], v_words[1] = gather_words(1)
        wa_second = large.tile([P, R_GROUPS, PACK, PASS], F32, name="large")
        for g in range(R_GROUPS):
            nc.sync.dma_start(
                wa_second[:, g], wa[PASS:, g * PASS : (g + 1) * PASS].rearrange("(p i) c -> p i c", i=PACK)
            )
            prepare_wa(1, g, wa_second[:, g])

        bring_load_chunk(0)
        for g in range(R_GROUPS):
            hidden(0, g)
        bring_load_chunk(1)
        wc_rows = held("wc_rows", [P, R_GROUPS, PACK, N], F32)
        for g in range(R_GROUPS):
            nc.sync.dma_start(wc_rows[:, g], wc[g * PASS : (g + 1) * PASS, :].rearrange("(p t) n -> p t n", t=PACK))
        prepare_wc(0)
        d_sb = held("d_sb", [P, PAGES], F32)
        with nc.allow_non_contiguous_dma(reason="one bias value a partition and page"):
            nc.sync.dma_start(d_sb[:], d.rearrange("(i p) -> p i", p=P))
        late_load = large.tile([P, R_GROUPS, PACK, S // 2], F32, name="large")
        bring_load(CHUNKS // 2, [late_load[:, g] for g in range(R_GROUPS)])
        prepare_wc(1)
        nc.sync.dma_start(wgo_sb[:, S // 2 :], wgo[:, S // 2 :])

        pages = [held("page%d" % i, [P, T2], F32) for i in range(PAGES)]
        for page in pages[:-1]:
            nc.vector.memset(page[:], 0.0)
        nc.gpsimd.memset(pages[-1][:], 0.0)

        last = CHUNKS - 1
        for c in range(last):
            for g in range(R_GROUPS):
                hidden(c + 1, g)
            score([(0, c), (1, c)])
            if c < last - 1:
                score([(2, c), (3, c)])
        score([(0, last), (1, last)])
        for i in (2, 3):
            score([(i, last - 1), (i, last)])
